import numpy as np, ml_dtypes
CORES = [16,18,20,22]
N = 4
BF = ml_dtypes.bfloat16
def gentries(a):
    return np.ascontiguousarray(a.reshape(8, 16, -1).transpose(0, 2, 1)).reshape(8, -1)
def gtable(e):
    e = np.asarray(e); return np.ascontiguousarray(e.reshape(8, -1, 16).transpose(0, 2, 1)).reshape(128, -1).astype(np.int32)
A, H, S, ST, RO, R = 1024, 4096, 128, 6, 3, 12
def atoms(rng, reach):
    off = np.concatenate([np.arange(-reach, 0), np.arange(1, reach + 1)])
    ch = off[np.argsort(rng.random((8, A, 2 * reach)), axis=-1)[..., :16]]
    ch = ch * (rng.random((8, A, 1)) >= 0.03125)
    pos = (np.arange(A)[None, :, None] + ch) % A
    nb = np.zeros((8, 16, A), np.int64)
    for g in range(8):
        o = rng.permutation(A); nb[g][:, o] = o[pos[g]].T
    return nb
def parts(rng, reach=R):
    nb = atoms(rng, reach); e = rng.integers(0, 256, (N, 8, 16, H)); s0 = rng.integers(0, A, (N, 8, RO, S))
    return nb, e, s0, rng.integers(0, 256, (N, 8, 16, S)), rng.integers(70 * ST, 210 * ST, (N, 8, 16))
def layers(rng):
    m = (A - 1) // (2 * ST - 1); lay = rng.permutation(A - 1)[:m * (2 * ST - 1)].reshape(2 * ST - 1, m); nb = rng.integers(0, A, (16, A))
    nb[:8, lay[0]] = rng.choice(lay[1], (8, m)); nb[8:, lay[0]] = rng.choice(lay[ST], (8, m))
    for i in range(1, 2 * ST - 1):
        nb[:, lay[i]] = A - 1 if i in (ST - 1, 2 * ST - 2) else rng.choice(lay[i + 1], (16, m))
    return nb, lay[0]
def owned(rng):
    n = 2 * ST; free = np.ones(A, bool); taken = np.zeros(H, bool); c = np.zeros((S, n), np.int64)
    for j in range(S):
        for m in range(n):
            x = rng.permutation(np.flatnonzero(free)); hs = []
            if m >= 2: hs.append(place(c[j, m - 2], c[j, m - 1], x))
            if m == n - 1: hs += [place(c[j, m - 1], x, c[j, 0]), place(x, c[j, 0], c[j, 1])]
            good = np.ones(x.shape, bool)
            for a in range(len(hs)):
                good &= ~taken[hs[a]]
                for b in range(a): good &= hs[a] != hs[b]
            i = int(np.argmax(good)); c[j, m] = x[i]; free[x[i]] = False
            for h in hs: taken[h[i]] = True
    nb = rng.integers(0, A, (16, A)); nb[:8, c[:, 0]] = c[:, 1]; nb[8:, c[:, 0]] = c[:, n - 1]
    for m in range(1, ST):
        nb[:, c[:, m]] = c[:, m + 1]; nb[:, c[:, n - m]] = c[:, n - m - 1]
    return nb, c[:, 0]
def pack(nb, e, s0, q, th):
    return {"nb": np.repeat(nb.reshape(1, 128, A), N, axis=0).astype(np.int32), "ang": e.reshape(N, 128, H).astype(np.float32).astype(BF),
            "st": np.stack([gtable(a.reshape(8, -1)) for a in s0]), "q": q.reshape(N, 128, S).astype(np.float32).astype(BF), "th": th.reshape(N, 128, 1).astype(np.int32)}
def setup_inputs(rng):
    return pack(*parts(rng))
def setup_inputs_ties(rng):
    nb, e, s0, q, th = parts(rng); v = np.arange(A)[None, :]
    nb[0] = 8 * (v >> 3) + rng.integers(0, 8, (16, A)); e[:, 0] = rng.choice(np.array([0, 192, 255, 255, 255]), (N, 1, H)); q[:, 0] = 0
    e[:, 1] = 10 * rng.integers(0, 2, (N, 16, H)); q[:, 1] = 10 * rng.integers(0, 2, (N, 16, S)); th[:, 1] = 10 * rng.integers(1, ST + 1, (N, 16))
    e[:, 2] = rng.choice(np.array([0, 3, 4, 255]), (N, 1, H)); q[:, 2] = 4; th[:, 2] = rng.integers(255, 520, (N, 1))
    e[:, 3] = 7; q[:, 3] = rng.integers(0, 256, (N, 16, S)); th[:, 3] = 7 * rng.integers(3, 2 * ST, (N, 16))
    e[:, 4] = rng.choice(np.array([100, 156]), (N, 16, H)); q[:, 4] = 128
    e[:, 5] = e[:, 5] * rng.integers(0, 2, (N, 16, H))
    for r in range(N):
        for g, n in ((5, 9), (6, 8), (7, 16)): th[r, g] = np.where(rng.permutation(16) < n, 0, 4095)
    return pack(nb, e, s0, q, th)
def setup_inputs_repeats(rng):
    nb, e, s0, q, th = parts(rng, 8)
    s0[:, ::2] = rng.choice(np.array([0, A - 1, A // 2, 5]), (N, 4, RO, S))
    e[:, 1::2] = e[:1, 1::2].copy(); q[:, 2::4] = q[:, 2::4, :, :1].copy()
    return pack(nb, e, s0, q, th >> 1)
def setup_inputs_stuck(rng):
    nb, e, s0, q, th = parts(rng); v = np.arange(A)[None, :]; k = np.arange(16)[:, None]
    nb[0] = 4 * (v >> 2) + rng.integers(0, 4, (16, A))
    nb[1, :8] = v; nb[2, 8:] = v
    nb[3] = v ^ rng.integers(0, 2, (16, A)); nb[3, ::8] = v ^ 1; nb[4] = v
    nb[5] = nb[5][rng.integers(0, 4, (16, A)), np.repeat(v, 16, axis=0)]
    nb[6] = 8 * (v >> 3) + rng.integers(0, 8, (16, A))
    x = v & 127; nb[7] = np.where(x == 0, v + 16 + k, np.where((x < 16) | (x >= 16 * (ST - 2)), v - x, v + 16))
    for g in (0, 3, 4, 6): th[:, g] = rng.integers(0, 800, (N, 16))
    s0[:, :, :, 0] = 0; s0[:, :, :, S - 1] = A - 1
    s0[:, 7] = 128 * rng.integers(0, A >> 7, (N, RO, S)) + rng.integers(1, 16, (N, RO, S))
    s0[0, 3] = rng.integers(256, A, (RO, 1)); th[0, 3] = 0
    return pack(nb, e, s0, q, th)
def setup_inputs_far(rng):
    nb, e, s0, q, th = parts(rng)
    for g in range(8):
        nb[g], a = layers(rng); s0[:, g] = rng.choice(a, (N, RO, S))
    if 2 * ST * S <= A:
        nb[1], a = owned(rng); s0[:, 1] = a[np.argsort(rng.random((N, RO, S)), axis=-1)]
    th = rng.integers(200 * ST, 300 * ST, (N, 8, 16)); th[2:, 5] = 4095; th[2:, 6] = 0; th[:2] = 0
    e[:, 2] = rng.integers(224, 256, (N, 16, H)); th[:, 2] = rng.integers(min(2048, 448 * ST), 448 * ST + 1, (N, 16))
    e[:, 3] = 255; th[:, 3] = 510 * ST; th[2:, 3, :8] = 510 * ST + 1
    return pack(nb, e, s0, q, th)
def setup_inputs_spread(rng):
    nb, e, s0, q, th = parts(rng); v = np.arange(A)[None, :]; k = np.arange(16)[:, None]
    e = (np.exp2(8 * rng.random((N, 8, 1, H))) * rng.random((N, 8, 16, H))).astype(np.int64)
    q = (np.exp2(8 * rng.random((N, 8, 1, S))) * rng.random((N, 8, 16, S))).astype(np.int64)
    th = np.minimum(np.exp2(12 * rng.random((N, 8, 16))).astype(np.int64), 4095)
    s0 = np.minimum((A * rng.random((N, 8, RO, S)) ** 3).astype(np.int64), A - 1)
    c = v & 3; nb[0] = 4 * rng.integers(0, A >> 2, (16, A)) + np.where(c >= 2, c, np.where(k < 8, 2, 3))
    s0[:, 0] = 4 * (s0[:, 0] >> 2) + rng.integers(0, 2, (N, RO, S))
    nb[2:4] = rng.integers(0, A, (2, 16, A))
    return pack(nb, e, s0, q, th)
def check_inputs(d):
    bad = []
    for k, lo, hi in (("nb", 0, A - 1), ("ang", 0, 255), ("st", 0, A - 1), ("q", 0, 255), ("th", 0, 4095)):
        v = np.asarray(d[k]).astype(np.float64)
        if not np.all((v >= lo) & (v <= hi)): bad.append("range of " + k)
        elif not np.all(v == np.floor(v)): bad.append(k + " holds numbers that aren't whole")
    if np.any(d["nb"] != d["nb"][:1]): bad.append("nb isn't alike on all ranks")
    return bad
def place(p, v, n):
    return ((((2 * p + 1) * (2 * n + 1)) >> 4) + 37 * v) & (H - 1)
def walk(e, v0, w, rows, nbr):
    path = [v0]; kk = np.arange(16)[None, :, None]
    for i in range(ST):
        v = path[i]; p = path[max(i - 1, 0)]
        n = np.take_along_axis(nbr, v[:, None, :], 2)
        h = place(p[:, None, :], v[:, None, :], n)
        x = np.take_along_axis(e, h.reshape(8, 1, 16 * S), 2).reshape(8, 16, 16, S)
        sc = np.add.reduce(np.abs(x - w[:, :, None, :]), axis=1)
        bar = np.any(np.stack(path)[:, :, None, :] == n[None], axis=0)
        if i == 0: bar = bar | (kk < rows) | (kk >= rows + 8)
        sc = np.where(bar, 2 ** 20, sc); k = np.argmin(sc, axis=1)[:, None, :]
        ok = np.take_along_axis(sc, k, 1)[:, 0] < 2 ** 20
        path.append(np.where(ok, np.take_along_axis(n, k, 1)[:, 0], v))
    return np.stack(path)
def reference(nb, ang, st, q, th):
    e = np.asarray(ang, np.float32).astype(np.int32).reshape(N, 8, 16, H); w = np.asarray(q, np.float32).astype(np.int32).reshape(N, 8, 16, S)
    lim = th.astype(np.int64).reshape(N, 8, 16, 1); nbr = nb.astype(np.int64).reshape(N, 8, 16, A)
    sl = np.stack([gentries(a) for a in st]).astype(np.int64).reshape(N, 8, RO, S)
    rings = np.zeros((N, 8, 16, RO, S), np.int64); m = np.arange(16)[None, :, None]
    for t in range(RO):
        new = []
        for r in range(N):
            s = (r + 1 + t % (N - 1)) % N
            pa = walk(e[r], sl[r, :, t], w[r], 0, nbr[r]); pb = walk(e[s], sl[r, :, t], w[r], 8, nbr[s])
            eq = pa[1:, None] == pb[None, 1:]; eq[0, 0] = False
            eq = eq.reshape(ST * ST, 8, S); found = np.any(eq, axis=0); f = np.argmax(eq, axis=0)
            i = f // ST + 1; j = f - (i - 1) * ST + 1; ln = np.where(found, i + j, 0)[:, None, :]; i = i[:, None, :]
            ca = np.take_along_axis(pa.transpose(1, 0, 2), np.minimum(m, i), 1); cb = np.take_along_axis(pb.transpose(1, 0, 2), np.clip(ln - m, 0, ST), 1)
            c = np.where(m <= i, ca, cb); live = m < ln
            before = np.take_along_axis(c, np.clip(np.where(m == 0, ln - 1, m - 1), 0, 15), 1)
            after = np.take_along_axis(c, np.clip(np.where(m == ln - 1, 0, m + 1), 0, 15), 1)
            h = place(before, c, after)
            x = np.take_along_axis(e[r], h.reshape(8, 1, 16 * S), 2).reshape(8, 16, 16, S)
            tot = np.add.reduce(np.where(live[:, None], x, 0), axis=2)
            heavy = found & (np.add.reduce((tot >= lim[r]).astype(np.int64), axis=1) >= 9)
            use = live & heavy[:, None, :]; gg = np.broadcast_to(np.arange(8)[:, None, None], h.shape)
            mark = np.zeros((8, H), bool); mark[gg[use], h[use]] = True
            new.append(np.where(mark[:, None, :], e[r] - (e[r] >> 2), e[r])); rings[r, :, :, t] = np.where(live, c, -1)
        e = np.stack(new)
    return {"ye": e.reshape(N, 128, H).astype(np.float32).astype(BF), "yr": rings.reshape(N, 128, RO * S).astype(np.float32)}

from concourse.bass import DstId, RemoteDMATransfer
from concourse.mybir import AluOpType as O, ActivationFunctionType as F

N, RO, ST, NCH = 4, 3, 6, 2
NTS = 19
SCRATCH, SHAPE, WIDE, PLACE = {}, {}, {}, {}
SEMAPHORES = ["sv", "ss", "sp", "sg", "as0", "aq", "ar0", "ar1", "ar2", "loc"] + ["d%d" % i for i in range(16)]
QSEM = {"V": "sv", "S": "ss", "P": "sp", "G": "sg"}
POOL = {"float32": "poolf", "bfloat16": "poolb", "float16": "poolh", "int32": "pooli", "uint16": "poolu"}
APART = "stu sr0 sr1 sr2 qa qr0 qr1 qr2 sti thi".split()


def sb(name, shape, dtype="float32"):
    SCRATCH[name] = ("sbuf", shape, dtype)


def many(dtype, cols, names):
    for n in names.split():
        if cols > 768 or n in APART: sb(n, [128, cols], dtype); continue
        pool = SCRATCH.setdefault(POOL[dtype], ("sbuf", [128, 0], dtype)); PLACE[n] = (POOL[dtype], pool[1][1]); SHAPE[n] = [128, cols]; WIDE[n] = dtype in ("float32", "int32")
        pool[1][1] += -(-cols // 32) * 32


many("int32", 1024, "nbi"); many("float32", 1024, "NBO IDT"); many("bfloat16", 4112, "E"); many("bfloat16", 4096, "G4")
many("bfloat16", 128, "qa qr0 qr1 qr2"); many("int32", 24, "sti"); many("uint16", 24, "stu sr0 sr1 sr2"); many("int32", 1, "thi"); many("float32", 1, "thf")
many("int32", 8, "pci"); many("float32", 8, "pcf C8 Pick mcol"); many("float16", 8, "C8h"); many("bfloat16", 8, "B32 B16")
many("float32", 136, "CI S1 PermO SEG T1 T3"); many("bfloat16", 136, "BIGP BIGA BIGB crN crA crB"); many("float32", 128, "CG CR If I296f dA dB"); many("float32", 288, "JX SEGJ")
many("float16", 128, "Ih I64 I296 ShB ShA G0"); many("bfloat16", 128, "one m296 Ib nIb m4Ib m64Ib m256Ib p4Ib Blk EQG Dm S01 CR0")
many("float32", 16, "PHE PRE"); many("float32", 2, "half"); many("float16", 640, "SelJ"); many("bfloat16", 2048, "SelT")
many("bfloat16", 2048, "xC mC"); many("float32", 128, "tn0 tn1 OSC")
sb("AL2", [128, 8, 16]); sb("EQ", [128, 8, 36], "bfloat16"); many("float32", 288, "FJ"); many("float16", 128, "BLs PL PA0 CS"); many("int32", 128, "IR")
many("float32", 128, "TT LF APs HF"); many("bfloat16", 128, "FN L0 L1 i0 MA MA64 Lm MN ML hiB TH NH LOT HIT"); many("bfloat16", 640, "MB"); many("float16", 768, "PB")
many("bfloat16", 8192, "OHL THH"); many("float32", 520, "CT"); many("bfloat16", 512, "NM"); many("bfloat16", 256, "NM2"); many("float32", 384, "YR")
for _p in "AB":
    for _d, _c, _l in (("float32", 128, "n t1"), ("int32", 128, "t2 t3"), ("uint16", 128, "hu"), ("bfloat16", 2048, "x m"), ("bfloat16", 768, "mk"), ("float32", 136, "RM R2"),
                       ("bfloat16", 136, "NQ"), ("float16", 128, "SP RR RD"), ("uint16", 8, "li")):
        many(_d, _c, " ".join(n + _p for n in _l.split()))
    for _n in ("k", "n", "o1", "o2"): SCRATCH["p" + _n + _p] = ("psum", [128, 512], "float32")
for _t in range(RO):
    many("uint16", 128, "hu0%d" % _t); many("bfloat16", 128, "mk0%d" % _t); many("float32", 128, "NC%d OA%d OB%d" % (_t, _t, _t))
    sb("BL%d" % _t, [128, 8, 16]); sb("BR%d" % _t, [128, 8, 16])
SHAPE.update({k: s[1] for k, s in SCRATCH.items()})
PSUM = {k for k, s in SCRATCH.items() if s[0] == "psum"}
WIDE.update({k: s[2] in ("float32", "int32") for k, s in SCRATCH.items()})


def v(name, *idx):
    sh = SHAPE[name]; reg = []; n = 1; full = list(idx) + [slice(None)] * (len(sh) - len(idx)); off = PLACE[name][1] if name in PLACE else 0
    for i, (ix, d) in enumerate(zip(full, sh)):
        if isinstance(ix, slice):
            a, b, s = ix.indices(d); k = len(range(a, b, s)); reg.append((a, a + (k - 1) * s + 1, s))
            if i: n *= k
            if i == 1: full[i] = slice(a + off, a + off + (k - 1) * s + 1, s)
        else:
            reg.append((ix, ix + 1, 1))
    return (name, tuple(full), tuple(reg), n)


ALL = slice(None)


def c(name, a=None, b=None, s=None): return v(name, ALL, slice(a, b, s))


def row(name): return v(name, slice(0, 1), ALL)


def ap(T, w): return T[PLACE[w[0]][0] if w[0] in PLACE else w[0]][w[1]]


def overlap(r, q):
    for (a, b, s), (d, e, u) in zip(r, q):
        if a >= e or d >= b: return False
        if s == u and s > 1 and (a - d) % s: return False
    return True


def covers(r, q): return all(s == 1 and a <= d and b >= e for (a, b, s), (d, e, u) in zip(r, q))


def add(G, q, fn, R, W, dur, grp=None, sem=None):
    i = len(G["ops"]); deps = {}
    for w, isw in [(x, False) for x in R] + [(x, True) for x in W]:
        name, reg = w[0], w[2]; keep = []
        for e in G["acc"].get(name, ()):
            j, r2, w2, g2 = e
            if j == i: keep.append(e); continue
            same = G["ops"][j]["q"] == q and q in QSEM; ov = overlap(reg, r2); hit = None
            if name in PSUM and not same: hit = True
            elif name in PSUM and q == "P":
                if grp is None or grp != g2: hit = False
            elif ov and (isw or w2): hit = True
            if hit is not None: deps[j] = deps.get(j, False) or hit
            if not (isw and ov and covers(reg, r2) and grp is None): keep.append(e)
        keep.append((i, reg, isw, grp)); G["acc"][name] = keep
    G["ops"].append({"q": q, "fn": fn, "deps": deps, "dur": dur, "sem": sem, "to": W[0][0] if W else ""})
    return i


VC = 0.00083


def vcost(n, f): return max(64, n * f) * VC


def two(*ws): return all(not WIDE[w[0]] for w in ws)


def vtt(G, o, a, b, op):
    add(G, "V", lambda g, T: g.vector.tensor_tensor(ap(T, o), ap(T, a), ap(T, b), op), [a, b], [o], vcost(o[3], 1 if (a[0] in PSUM or b[0] in PSUM) else 2))


def vts(G, o, a, s1, op0, s2=None, op1=None):
    def fn(g, T):
        x = ap(T, s1) if isinstance(s1, tuple) else s1
        if op1 is None: return g.vector.tensor_scalar(ap(T, o), ap(T, a), x, None, op0)
        return g.vector.tensor_scalar(ap(T, o), ap(T, a), x, s2, op0, op1)
    add(G, "V", fn, [a] + ([s1] if isinstance(s1, tuple) else []), [o], vcost(o[3], 0.5 if two(o, a) else 1))


def vcp(G, o, a): add(G, "V", lambda g, T: g.vector.tensor_copy(ap(T, o), ap(T, a)), [a], [o], vcost(o[3], 0.5 if two(o, a) else 1))


def vscan(G, o, a, b, op0, op1):
    add(G, "V", lambda g, T: g.vector.tensor_tensor_scan(ap(T, o), ap(T, a), ap(T, b), 0.0, op0, op1), [a, b], [o], vcost(o[3], 0.5 if two(o, a, b) else 1))


def vset(G, o, x): add(G, "V", lambda g, T: g.vector.memset(ap(T, o), x), [], [o], vcost(o[3], 1))


def vgat(G, o, w, off):
    add(G, "V", lambda g, T: g.vector.tensor_copy(ap(T, o), ap(T, w).indirect(ap(T, off))), [w, off], [o], o[3] * VC * 1.5 + 0.05)


def act(G, o, a, func=F.Copy, bias=0.0, scale=1.0):
    add(G, "S", lambda g, T: g.scalar.activation(ap(T, o), ap(T, a), func, bias=bias, scale=scale), [a], [o], o[3] * VC + 0.02)


def gat(G, o, w, off):
    add(G, "S", lambda g, T: g.scalar.activation(ap(T, o), ap(T, w).indirect(ap(T, off)), F.Copy), [w, off], [o], o[3] * VC * 1.5 + 0.065)


def gather_all(G, x, hu):
    n = 128 // NCH
    for h in range(NCH): gat(G, c(x, 16 * n * h, 16 * n * (h + 1)), c("E"), c(hu, n * h, n * (h + 1)))


def mm(G, o, l, r, start=True, stop=True, grp=None):
    add(G, "P", lambda g, T: g.tensor.matmul(ap(T, o), ap(T, l), ap(T, r), start, stop), [l, r], [o], max(min(64, l[3]), r[3]) * (4 if WIDE[l[0]] else 1) * 0.0005, grp=grp)


def group(G, o, terms):
    for i, (l, r) in enumerate(terms): mm(G, o, l, r, i == 0, i == len(terms) - 1)


def iota(G, o, pat, base, cm, small=True):
    def fn(g, T):
        if small: return g.iota(ap(T, o), pat, base, cm, allow_small_or_imprecise_dtypes=True)
        return g.iota(ap(T, o), pat, base, cm)
    add(G, "G", fn, [], [o], 0.13 + o[3] * 2 * VC)


def dma(G, fn, R, W, dur):
    k = "d%d" % G["nd"][0]; G["nd"][0] += 1; add(G, "Y", fn, R, W, dur, sem=(k, 16))


LATER = {"mA": 2.0, "mB": 2.0, "mC": 2.0, "mkA": 2.0, "mkB": 2.0}


def schedule(G):
    ops = G["ops"]; n = len(ops); succ = [[] for _ in ops]; need = [0] * n
    for i, o in enumerate(ops):
        need[i] = len(o["deps"])
        for d in o["deps"]: succ[d].append(i)

    def lat(d, i): return 0.0 if not ops[i]["deps"][d] else (0.06 if ops[d]["q"] == ops[i]["q"] else 0.1)
    far = [0.0] * n; pr = [0.0] * n
    for i in range(n - 1, -1, -1):
        far[i] = ops[i]["dur"] + max([far[s] + lat(i, s) for s in succ[i]] + [0.0]); pr[i] = far[i] - LATER.get(ops[i]["to"], 0.0)
    free = {q: 0.0 for q in "VSPGYN"}; ready = {q: [] for q in free}; rt = [0.0] * n; order = []
    for i in range(n):
        if not need[i]: ready[ops[i]["q"]].append(i)
    while len(order) < n:
        best = None
        for q in free:
            if not ready[q]: continue
            t0 = max(free[q], min(rt[i] for i in ready[q]))
            i = max((j for j in ready[q] if rt[j] <= t0 + 1e-9), key=lambda j: (pr[j], -j))
            if best is None or t0 < best[0]: best = (t0, i)
        t0, i = best; q = ops[i]["q"]; ready[q].remove(i); order.append(i); end = t0 + ops[i]["dur"]; free[q] = end if q in QSEM else t0 + 0.1
        for s in succ[i]:
            rt[s] = max(rt[s], end + lat(i, s)); need[s] -= 1
            if not need[s]: ready[ops[s]["q"]].append(s)
        ops[i]["t"] = (t0, end)
    return order


def emit(G, order, g, T):
    ops = G["ops"]; eng = {"V": g.vector, "S": g.scalar, "P": g.tensor, "G": g, "Y": g.sync}
    clock = {q: {} for q in eng}; snap = {}; cnt = {q: 0 for q in QSEM}; done = {}
    for i in order:
        o = ops[i]; q = o["q"]
        if q == "N": done[i] = o["sem"]; snap[i] = {}; continue
        ck = clock[q]; want = {}
        for d, w in o["deps"].items():
            if w:
                s, x = done[d]
                if ck.get(s, 0) < x and want.get(s, (0, 0))[0] < x: want[s] = (x, d)
        for s, (x, d) in sorted(want.items(), key=lambda z: -z[1][1]):
            if ck.get(s, 0) >= x: continue
            eng[q].wait_ge(T.sem[s], x); ck[s] = x
            for s2, x2 in snap[d].items():
                if ck.get(s2, 0) < x2: ck[s2] = x2
        snap[i] = dict(ck); ins = o["fn"](g, T)
        if o["sem"] is not None:
            if q == "Y": ins.then_inc(T.sem[o["sem"][0]], o["sem"][1])
            done[i] = o["sem"]
        else:
            cnt[q] += 1; ins.then_inc(T.sem[QSEM[q]], 1); done[i] = (QSEM[q], cnt[q])
    for q in QSEM: g.wait_ge(T.sem[QSEM[q]], cnt[q])
    for k in range(G["nd"][0]): g.wait_ge(T.sem["d%d" % k], 16)


def constants(G):
    iota(G, c("pci", 0, 1), [[0, 1]], 0, 1, False)
    iota(G, c("CI"), [[1, 136]], 0, 0); iota(G, c("CG"), [[1, 8], [0, 16]], 0, 0); iota(G, c("CR"), [[0, 8], [1, 16]], 0, 0)
    iota(G, c("S1"), [[0, 8], [1, 17]], -1, 0); iota(G, c("JX"), [[0, 8], [1, 36]], 0, 0); iota(G, c("IDT"), [[2, 1024]], 1, 0)
    p = c("pci", 0, 1)
    for k, (x, op) in enumerate(((15, O.bitwise_and), (4, O.arith_shift_right), (7, O.bitwise_and), (3, O.arith_shift_right))): vts(G, c("pci", k + 1, k + 2), p, x, op)
    vcp(G, c("pcf", 0, 5), c("pci", 0, 5))
    P, PR, PG, P8, PH = [c("pcf", k, k + 1) for k in range(5)]
    vts(G, c("pcf", 5, 6), P, 1.0, O.add); vts(G, c("pcf", 6, 7), P, -1.0, O.add)
    vtt(G, c("pcf", 7, 8), P, PG, O.add); vts(G, c("pcf", 7, 8), c("pcf", 7, 8), 1.0, O.add)
    ci = c("CI", 0, 128); vts(G, c("If"), ci, P, O.is_equal); vts(G, c("Ib"), ci, P, O.is_equal)
    for nm, x in (("Ih", 1.0), ("I64", 64.0), ("I296", 296.0), ("I296f", 296.0)): vts(G, c(nm), c("If"), x, O.mult)
    for nm, x in (("nIb", -1.0), ("m4Ib", -4096.0), ("m64Ib", -64.0), ("m256Ib", -256.0), ("p4Ib", 4096.0)): vts(G, c(nm), c("Ib"), x, O.mult)
    vts(G, c("PRE"), c("CI", 0, 16), PR, O.is_equal); vts(G, c("PHE"), c("CI", 0, 16), PH, O.is_equal)
    ha, hb = c("half", 0, 1), c("half", 1, 2); vts(G, ha, PR, 7.5, O.is_le); vts(G, hb, PR, 7.5, O.is_ge)
    vts(G, c("dA"), c("If"), ha, O.mult); vts(G, c("dB"), c("If"), hb, O.mult)
    vts(G, c("Blk"), c("CG"), PG, O.is_equal); vts(G, c("EQG"), c("CG"), P8, O.is_equal); vts(G, c("Dm"), c("CR"), PR, O.is_equal)
    vts(G, c("S01"), c("CR"), 0.0, O.not_equal); vts(G, c("CR0"), c("CR"), 0.0, O.is_equal)
    vts(G, c("C8"), c("CI", 0, 8), PG, O.is_equal); vcp(G, c("C8h"), c("C8")); vts(G, c("B32"), c("C8"), 32.0, O.mult); vts(G, c("B16"), c("C8"), -16.0, O.mult)
    vts(G, c("Pick"), c("C8"), c("PRE", 0, 1), O.mult)
    vts(G, c("PermO"), c("CI"), c("pcf", 7, 8), O.is_equal); vts(G, c("BIGP"), c("PermO"), 262144.0, O.mult)
    vts(G, c("BIGA"), c("BIGP"), ha, O.mult); vts(G, c("BIGB"), c("BIGP"), hb, O.mult)
    vts(G, c("SEG"), c("S1"), -1.0, O.is_equal, 4194304.0, O.mult)
    r = row
    vts(G, r("T1"), r("S1"), -1.0, O.is_equal, 131073.0, O.mult); vtt(G, r("T1"), r("S1"), r("T1"), O.add); vcp(G, r("crN"), r("T1"))
    vts(G, r("T3"), r("S1"), 7.5, O.is_ge, 262144.0, O.mult); vtt(G, r("crA"), r("T1"), r("T3"), O.add)
    vts(G, r("T3"), r("S1"), 7.5, O.is_le, 262144.0, O.mult); vtt(G, r("T1"), r("T1"), r("T3"), O.add)
    vts(G, r("T3"), r("S1"), -0.5, O.is_le, -262144.0, O.mult); vtt(G, r("crB"), r("T1"), r("T3"), O.add)
    vset(G, row("one"), 1.0); vset(G, row("m296"), -296.0)
    vts(G, c("SEGJ"), c("JX"), 0.0, O.is_equal, -4096.015625, O.mult); vts(G, c("SEGJ"), c("SEGJ"), 0.015625, O.add)
    for j in range(6): vts(G, c("mcol", j, j + 1), PR, float(j), O.add)
    for j in range(1, 6): vts(G, c("SelJ", 128 * (j - 1), 128 * j), c("Blk"), c("PRE", j, j + 1), O.mult)
    for h in range(16): vts(G, c("SelT", 128 * h, 128 * h + 128), c("EQG"), c("PHE", h, h + 1), O.mult, 256.0, O.mult)
    vts(G, c("ShB"), ci, c("pcf", 5, 6), O.is_equal); vtt(G, c("ShB"), c("ShB"), c("S01"), O.mult)
    vts(G, c("ShA"), ci, c("pcf", 6, 7), O.is_equal); vtt(G, c("G0"), c("Blk"), c("CR0"), O.mult)
    for p_ in "AB": vset(G, c("SP" + p_), 0.0)
    vset(G, v("AL2"), 0.0); vset(G, v("EQ"), 0.0); vset(G, c("CT"), 0.0)
    for t in range(RO): vset(G, v("BL%d" % t), 0.0)
    vset(G, c("E", 4096, 4112), 0.0)
    for p_ in "AB": mm(G, c("pk" + p_, 144, 272), c("Ib"), c("Dm"))


def angles(G, p, n, P, Vp, hu):
    t1, t2, t3 = c("t1" + p), c("t2" + p), c("t3" + p)
    vtt(G, t1, n, P, O.mult); vtt(G, t2, t1, Vp, O.add); vts(G, t3, t2, 4, O.arith_shift_right, 4095, O.bitwise_and)
    if hu is not None: vcp(G, hu, t3)


def first(G, t):
    sa, sb_ = c("stu", 8 * t, 8 * t + 8), c("sr%d" % t, 8 * t, 8 * t + 8); oa, ob, nc = c("OA%d" % t), c("OB%d" % t), c("NC%d" % t); b = "pnB"
    gat(G, oa, c("IDT"), sa); gat(G, ob, c("IDT"), sb_); gat(G, c("tn0"), c("NBO"), sa); gat(G, c("tn1"), c("NBO"), sb_)
    group(G, c(b, 0, 128), [(c("dA"), oa), (c("dB"), ob)]); group(G, c(b, 128, 256), [(c("dA"), c("tn0")), (c("dB"), c("tn1"))])
    act(G, c("OSC"), c(b, 0, 128)); act(G, nc, c(b, 128, 256))
    group(G, c(b, 256, 384), [(c("I296f"), c("OSC")), (row("one"), row("m296"))])
    angles(G, "B", nc, c(b, 0, 128), c(b, 256, 384), c("hu0%d" % t)); vtt(G, c("mk0%d" % t), nc, c(b, 0, 128), O.is_equal)


def slot(p, i): return c("po1" + p, 128 * i, 128 * i + 128) if i < 4 else c("po2" + p, 128 * i - 512, 128 * i - 384)


def scores(G, p, a, t, xb, mb, ks):
    gid = ("key", p, a, t); col = lambda k: c("pk" + p, k + 1, 136, 17); mx = lambda k: c(mb, 128 * k, 128 * k + 128)
    mm(G, c("pk" + p, 0, 136), row("one"), row("crN") if a else row("cr" + p), True, False)
    for l, r in [(c("mk" + p, 128 * i, 128 * i + 128), c("BIGP")) for i in range(a + 1)] if a else [(c("mk0%d" % t), c("BIG" + p))]:
        mm(G, c("pk" + p, 0, 136), l, r, False, False, grp=gid)
    for k in ks: mm(G, col(k), c(xb, k, 2048, 16), c("B16"), False, False, grp=gid)
    for k in ks[:-1]: mm(G, col(k), mx(k), c("B32"), False, False, grp=gid)
    mm(G, col(ks[-1]), mx(ks[-1]), c("B32"), False, True)


def maxima(G, xb, mb, who):
    n = 128 // NCH
    for h in range(0, 128, n):
        for k in range(16): vtt(G, c(mb, 128 * k + h, 128 * k + h + n), c(xb, 16 * h + k, 16 * (h + n), 16), c("po2" + who(k), 384 + h, 384 + h + n), O.max)


def choose(G, p, a, t):
    key = c("pk" + p, 0, 136); pn = c("pn" + p, 0, 136); R2 = c("R2" + p); RR = c("RR" + p); fin = c("R2" + p, 16, 136, 17)
    vscan(G, c("RM" + p), c("SEG"), key, O.add, O.min); vtt(G, c("NQ" + p), c("RM" + p), key, O.not_equal)
    mm(G, pn, c("m4Ib"), c("NQ" + p), False, True)
    vscan(G, R2, c("NQ" + p), pn, O.mult, O.max)
    if a < ST - 1:
        vcp(G, c("SP" + p, 0, 128, 16), fin); vscan(G, RR, c("S01"), c("SP" + p), O.mult, O.add)
        vtt(G, c("RD" + p), RR, c("pk" + p, 144, 272), O.mult)
        mm(G, c("pk" + p, 136, 144), c("RD" + p), c("C8h")); vts(G, c("li" + p), c("pk" + p, 136, 144), 0.5, O.mult, -0.5, O.add)
        mm(G, slot(p, a + 1), RR, c("Ih"))
        group(G, c("po2" + p, 256, 384), [(RR, c("I296")), (row("one"), row("m296"))])
    act(G, v("AL2" if p == "A" else "BL%d" % t, ALL, ALL, a + 1), fin)


def names(G, p, a, t):
    pn = c("pn" + p, 0, 136); s0 = c("pn" + p, 0, 136, 17)
    mm(G, pn, c("n" + p) if a else c("NC%d" % t), c("PermO"), True, False)
    if a: mm(G, s0, c("If"), c("R2" + p, 16, 136, 17), False, False)
    else: mm(G, s0, c("O%s%d" % (p, t)), c("Pick"), False, False)


def walk(G, t):
    for p in "AB":
        mm(G, c("po2" + p, 384, 512), c("Ib"), c("qa") if p == "A" else c("qr%d" % t)); mm(G, slot(p, 0), c("If"), c("O%s%d" % (p, t)))
    mm(G, c("pnA", 144, 152), c("OA%d" % t), c("Pick")); act(G, v("AL2", ALL, ALL, 0), c("pnA", 144, 152))
    for p in "AB": names(G, p, 0, t)
    gather_all(G, "xC", "hu0%d" % t); maxima(G, "xC", "mC", lambda k: "A" if k < 8 else "B")
    scores(G, "A", 0, t, "xC", "mC", list(range(8))); scores(G, "B", 0, t, "xC", "mC", list(range(8, 16)))
    for p in "AB": choose(G, p, 0, t)
    for a in range(1, ST):
        for p in "AB":
            vgat(G, c("n" + p), c("NBO"), c("li" + p))
            angles(G, p, c("n" + p), slot(p, a - 1), c("po2" + p, 256, 384), c("hu" + p))
            gather_all(G, "x" + p, "hu" + p); names(G, p, a, t)
            for i in range(a + 1): vtt(G, c("mk" + p, 128 * i, 128 * i + 128), c("n" + p), slot(p, i), O.is_equal)
            maxima(G, "x" + p, "m" + p, lambda k, p=p: p); scores(G, p, a, t, "x" + p, "m" + p, list(range(16))); choose(G, p, a, t)


def rings(G, t):
    al = lambda a, b: v("AL2", ALL, ALL, slice(a, b)); br = lambda a, b: v("BR%d" % t, ALL, ALL, slice(a, b))
    for d in range(-5, 6):
        i0 = max(1, 1 + d) if d else 2; i1 = min(6, 6 + d); n = i1 - i0 + 1; f0 = (i0 - 1) * 6 + i0 - d - 1
        vtt(G, v("EQ", ALL, ALL, slice(f0, f0 + 7 * (n - 1) + 1, 7)), al(i0, i1 + 1), br(i0 - d, i1 - d + 1), O.is_equal)
    mm(G, c("pnA", 0, 288), c("Ib"), v("EQ"))
    vscan(G, c("FJ"), c("SEGJ"), c("pnA", 0, 288), O.add, O.max)
    vcp(G, c("SPA", 0, 128, 16), c("FJ", 35, 288, 36)); vscan(G, c("RRA"), c("S01"), c("SPA"), O.mult, O.add)
    y = c("pnB", 0, 128); mm(G, y, c("RRA"), c("I64"))
    AL1, BL1 = c("po1B", 0, 128), c("po1B", 128, 256); mm(G, AL1, v("AL2"), c("If")); mm(G, BL1, v("BR%d" % t), c("If"))
    vcp(G, c("BLs"), BL1); brep = [c("po2B", 128 * j, 128 * j + 128) for j in range(4)] + [c("po1B", 256, 384)]
    for j in range(5): mm(G, brep[j], c("SelJ", 128 * j, 128 * j + 128), c("BLs"))
    vts(G, c("IR"), y, -1.0 / 6, O.mult, 17.0 + 1.0 / 12, O.add); vts(G, c("TT"), c("IR"), -5.0, O.mult, 106.0, O.add)
    vtt(G, c("LF"), c("TT"), y, O.subtract); vts(G, c("FN"), y, 63.5, O.is_ge); vtt(G, c("L0"), c("LF"), c("FN"), O.mult)
    vts(G, c("L1"), c("L0"), -1.0, O.add); vtt(G, c("i0"), c("IR"), c("L1"), O.min)
    m = lambda j: c("mcol", j, j + 1)
    vts(G, c("MA"), c("i0"), m(0), O.is_ge); vts(G, c("MA64"), c("i0"), m(0), O.is_ge, 64.0, O.mult)
    vtt(G, c("Lm"), c("L0"), c("MA64"), O.subtract); vts(G, c("MN"), c("L0"), m(0), O.is_le); vts(G, c("ML"), c("L0"), m(1), O.is_equal)
    vtt(G, c("PB", 0, 128), c("MA"), AL1, O.mult)
    for j in range(1, 6):
        mb = c("MB", 128 * j - 128, 128 * j); vts(G, mb, c("Lm"), m(j), O.is_equal); vtt(G, c("PB", 128 * j, 128 * j + 128), mb, brep[j - 1], O.mult)
    CP = c("pkB", 0, 128)
    group(G, CP, [(c("nIb"), c("MN"))] + [(c("Ih"), c("PB", 128 * j, 128 * j + 128)) for j in range(6)])
    vcp(G, c("CS"), CP); act(G, c("YR", 128 * t, 128 * t + 128), CP, F.Identity, -0.5, 0.5)
    vtt(G, c("PL"), c("ML"), CP, O.mult); vtt(G, c("PA0"), c("ML"), slot("A", 0), O.mult)
    BP, AP, VP, NN = [c("pnA", 128 * j, 128 * j + 128) for j in range(4)]
    group(G, NN, [(c("p4Ib"), c("MN"))]); group(G, VP, [(c("I296"), c("CS")), (row("one"), row("m296"))])
    group(G, AP, [(c("Ih"), c("PA0")), (c("Ib"), c("ML")), (c("ShA"), c("CS"))]); group(G, BP, [(c("ShB"), c("CS")), (c("G0"), c("PL"))])
    act(G, c("APs"), AP)
    angles(G, "A", c("APs"), BP, VP, None); vtt(G, c("HF"), c("t3A"), NN, O.max); vcp(G, c("huA"), c("HF"))
    gather_all(G, "xA", "huA")
    vts(G, c("hiB"), c("HF"), 1.0 / 64, O.mult, 129.0 - 63.0 / 128, O.add)
    LO = c("pkB", 272, 400); group(G, LO, [(c("HF"), c("If")), (c("hiB"), c("m64Ib"))]); vts(G, c("LOT"), LO, 8256.0, O.add)
    for u in range(64): vts(G, c("OHL", 128 * u, 128 * u + 128), c("LOT"), float(u), O.is_equal)
    tot = c("pnB", 128, 256); group(G, tot, [(c("Ib"), c("xA", k, 2048, 16)) for k in range(12)])
    vts(G, c("TH"), tot, c("thf"), O.is_ge); cnt = c("pnB", 256, 384); mm(G, cnt, c("Blk"), c("TH")); vts(G, c("NH"), cnt, 8.5, O.is_le)
    HI = c("po1B", 384, 512); group(G, HI, [(c("hiB"), c("Ib")), (c("MN"), c("m256Ib")), (c("NH"), c("m256Ib"))]); act(G, c("HIT"), HI, F.Identity, -129.0)


def lessen(G, t):
    for u in range(64):
        o = c("THH", 128 * u, 128 * u + 128)
        if u < NTS: act(G, o, c("HIT"), F.Sigmoid, -200.0 * (u - 0.5), 200.0)
        else: vts(G, o, c("HIT"), float(u), O.is_ge)
    lo64 = slice(0, 64)
    for g in range(8): group(G, v("po2A", lo64, slice(g, 512, 8)), [(c("OHL", 16 * g + m, 8192, 128), c("THH", 16 * g + m, 8192, 128)) for m in range(12)])
    pc = v("po2A", lo64, slice(0, 512)); act(G, v("CT", lo64, slice(0, 512)), pc); vtt(G, v("NM", lo64, ALL), v("CT", lo64, slice(8, 520)), pc, O.is_equal)
    for b in range(4): mm(G, c("pnA", 64 * b, 64 * b + 64), v("NM", lo64, slice(128 * b, 128 * b + 128)), v("Ib", lo64, slice(0, 64)))
    act(G, c("NM2"), c("pnA", 0, 256), F.Identity, 0.5, 2.0)
    for k in range(8):
        bank = ("po2B", "pnB", "po1A", "pkA", "po1B")[k % 5]; e = c("E", 512 * k, 512 * k + 512); o = c(bank, 0, 512); b = k // 2
        mm(G, o, c("Ib"), e, True, False); mm(G, o, c("nIb"), c("G4", 512 * k, 512 * k + 512), False, False)
        for h in range(8):
            s = 128 * ((k % 2) * 8 + h); mm(G, c(bank, 64 * h, 64 * h + 64), c("SelT", s, s + 128), c("NM2", 64 * b, 64 * b + 64), False, h == 7)
        vtt(G, e, e, o, O.min)
        if t == RO - 1 and k % 2:
            a = 512 * (k - 1); dma(G, lambda g, T, a=a: g.sync.dma_start(T.ye[:, a:a + 1024], T.E[:, a:a + 1024]), [c("E", a, a + 1024)], [], 3.5)
    if t < RO - 1:
        quarter(G); mm(G, c("pkA", 144, 272), c("Ib"), c("Dm"))


def quarter(G):
    for k in range(8): act(G, c("G4", 512 * k, 512 * k + 512), c("E", 512 * k, 512 * k + 512), F.Identity, 127.625, 0.25)


def build(rank, core, topo):
    G = {"ops": [], "acc": {}, "nd": [0]}; peers = [(rank + 1 + t) % N for t in range(RO)]; asks = [(rank - 1 - t) % N for t in range(RO)]; ne = 8

    def eng(T, dst):
        m = 0
        for e in topo.engines(core, T.cores[dst])[:ne]: m |= 1 << e
        return m

    def did(T, dst):
        a = topo.addr(T.cores[dst]); return DstId(rid=a[0], pnc=a[1])

    def send3(src, dsts, sem):
        def fn(g, T):
            return g.remote_dma_fused([RemoteDMATransfer(dst_ids=[did(T, s) for s in peers], dma_engine_mask=eng(T, peers[0]), remote_sem=T.sem[sem],
                                                         srcs=[T[src][:]], dsts=[T[d][:] for d in dsts], alu_op=0)], local_sem=T.sem.loc)
        return fn
    dma(G, lambda g, T: g.sync.dma_start(T.sti[:], T.st[:]), [], [c("sti")], 2.0)
    dma(G, lambda g, T: g.sync.dma_start(T.qa[:], T.q[:]), [], [c("qa")], 2.0)
    dma(G, lambda g, T: g.sync.dma_start(T.nbi[:], T.nb[:]), [], [c("nbi")], 4.0)
    dma(G, lambda g, T: g.sync.dma_start(T.E[:, 0:4096], T.ang[:]), [], [c("E", 0, 4096)], 8.0)
    dma(G, lambda g, T: g.sync.dma_start(T.thi[:], T.th[:]), [], [c("thi")], 2.0)
    vcp(G, c("stu"), c("sti"))
    s1 = add(G, "G", send3("stu", ["sr0", "sr1", "sr2"], "as0"), [c("stu")], [], 1.0, sem=("loc", 0))
    s2 = add(G, "G", send3("qa", ["qr0", "qr1", "qr2"], "aq"), [c("qa")], [], 1.0, sem=("loc", 0))
    for s, nm, sem in ((s1, "sr", "as0"), (s2, "qr", "aq")):
        i = add(G, "N", None, [], [c(nm + "%d" % t) for t in range(RO)], 3.0, sem=(sem, 3 * ne)); G["ops"][i]["deps"][s] = False
    constants(G)
    vts(G, c("NBO"), c("nbi"), 2.0, O.mult, 1.0, O.add); vcp(G, c("thf"), c("thi"))
    first(G, 0); quarter(G)
    for t in range(RO):
        walk(G, t)

        def back(g, T, t=t):
            a = topo.addr(T.cores[asks[t]])
            return g.remote_dma(T["BR%d" % t][:], T["BL%d" % t][:], T.sem["ar%d" % t], T.sem.loc, a[1], a[0], eng(T, asks[t]))
        s = add(G, "G", back, [v("BL%d" % t)], [], 0.5, sem=("loc", 0))
        i = add(G, "N", None, [], [v("BR%d" % t)], 2.5, sem=("ar%d" % t, ne)); G["ops"][i]["deps"][s] = False
        if t < RO - 1: first(G, t + 1)
        rings(G, t); lessen(G, t)
    dma(G, lambda g, T: g.sync.dma_start(T.yr[:], ap(T, c("YR"))), [c("YR")], [], 3.0)
    return G, ne


def rank_program(g, core, T, topo):
    rank = T.rank_of(core)
    if rank is None: return
    G, ne = build(rank, core, topo); emit(G, schedule(G), g, T)
    g.wait_ge(T.sem.loc, ne * (2 + RO))
